import numpy as np
import ml_dtypes


def mxq(x, axis, fmt="e4m3"):
    dtype, down = {"e4m3": (ml_dtypes.float8_e4m3fn, 7), "e5m2": (ml_dtypes.float8_e5m2, 14)}[fmt]
    v = np.moveaxis(np.asarray(x, np.float32).astype(ml_dtypes.bfloat16).astype(np.float64), axis, -1)
    blocks = v.reshape(v.shape[:-1] + (-1, 32))
    amax = np.abs(blocks).max(-1, keepdims=True)
    byte = np.maximum(np.where(amax > 0, np.frexp(amax)[1] - 1 + 127, 0) - down, 1)
    scale = np.exp2(byte - 127.0)
    codes = (blocks / scale).astype(np.float32).astype(dtype).astype(np.float64)
    return np.moveaxis((codes * scale).reshape(v.shape), -1, axis)


WIDE = False


def mx_kscale(k):
    if not WIDE:
        return np.ones(k)
    levels = np.array([10, -10, 5, -5, 0])
    if k % 512:
        return np.exp2(np.random.permutation(np.resize(levels, k // 32))).repeat(32)
    a = np.empty((k // 512, 16))
    for p in range(k // 512):
        a[p, :8] = np.random.permutation(np.resize(levels, 8))
        for g in range(8):
            far = levels[np.abs(levels - a[p, g]) >= 10]
            a[p, g + 8] = far[np.random.randint(len(far))]
    return np.exp2(a.ravel()).repeat(32)


def f64(x):
    return np.asarray(x).astype(np.float64)


def striped(idx):
    return np.tile(np.asarray(idx).reshape(-1, 16).T, (8, 1)).astype(np.uint16)


def unstriped(offs):
    return offs[:16].T.reshape(-1).astype(np.int64)


E2M1 = np.array([0.0, 0.5, 1.0, 1.5, 2.0, 3.0, 4.0, 6.0, -0.0, -0.5, -1.0, -1.5, -2.0, -3.0, -4.0, -6.0])


def pack_weight(w, fmt):
    k, n = w.shape
    w = f64(np.asarray(w, np.float32).astype(ml_dtypes.bfloat16)).reshape(k // 32, 32, n)
    amax = np.abs(w).max(1)
    if fmt == "e4m3":
        byte = np.frexp(amax)[1] - 1 + 127 - 7
    else:
        mant, ex = np.frexp(amax / 6.0)
        byte = np.where(mant > 0.5, ex, ex - 1) + 127
    byte = np.clip(np.where(amax > 0, byte, 1), 1, 254)
    scaled = (w * np.exp2(127.0 - byte)[:, None, :]).reshape(k, n).astype(np.float32)
    by_word = np.ascontiguousarray(scaled.reshape(k // 512, 128, 4, n).transpose(0, 1, 3, 2))
    if fmt == "e4m3":
        words = by_word.astype(ml_dtypes.float8_e4m3fn).view(np.uint8)
    else:
        c = by_word.astype(ml_dtypes.float4_e2m1fn).view(np.uint8) & 0xF
        words = (c[..., 0::2] | (c[..., 1::2] << 4)).reshape(k // 512, 128, 2 * n)
    return np.ascontiguousarray(words), np.ascontiguousarray(byte.astype(np.uint8).reshape(k // 512, 16, n))


def unpack_weight(words, scales, fmt):
    g, _, n = scales.shape
    words = np.ascontiguousarray(words).reshape(g, 128, n, -1)
    if fmt == "e4m3":
        vals = words.view(ml_dtypes.float8_e4m3fn).astype(np.float64)
    else:
        nib = np.empty((g, 128, n, 4), np.uint8)
        nib[..., 0::2] = words & 0xF
        nib[..., 1::2] = words >> 4
        vals = E2M1[nib]
    vals = vals * np.repeat(np.exp2(scales.astype(np.float64) - 127.0), 8, axis=1)[..., None]
    return vals.transpose(0, 1, 3, 2).reshape(g * 512, n)


def sigmoid(v):
    return 1.0 / (1.0 + np.exp(-v))


D, E, T, I, Q = 512, 512, 1024, 256, 512


def setup_inputs():
    n = np.random.standard_normal
    idx = np.random.permutation(T)[:I]
    fd = mx_kscale(D)
    fq = mx_kscale(Q)
    keysp = pack_weight(n((D, T)) / fd[:, None], "e4m3")
    return {
        "query": (n((D, Q)) * 0.5 / np.sqrt(D) * fd[:, None]).astype(np.float32),
        "query2": (n((D, Q)) * 0.8 / np.sqrt(D) * fd[:, None]).astype(np.float32),
        "keys_words": keysp[0],
        "keys_scales": keysp[1],
        "size": (np.random.uniform(0.5, 2.0, (1, I))).astype(np.float32),
        "qs": (np.random.uniform(2.0, 8.0, (Q, 1)) * fq[:, None]).astype(np.float32),
        "grows": (n((Q, E)) / fq[:, None]).astype(np.float32),
        "old": (n((E, T)) * 2.0).astype(np.float32),
        "fade": (np.random.uniform(0.5, 1.0, (1, T))).astype(np.float32),
        "offs": striped(idx),
    }


def reference(query, query2, keys_words, keys_scales, size, qs, grows, old, fade, offs):
    idx = unstriped(offs)
    keysu = unpack_weight(keys_words, keys_scales, "e4m3")
    queryq = mxq(f64(query), 0, "e4m3")
    keysidxg = keysu[:, idx]
    a = queryq.T @ keysidxg
    query2q = mxq(f64(query2), 0, "e4m3")
    b = query2q.T @ keysidxg
    r = np.exp(a - np.max(a, axis=1, keepdims=True))
    gt = sigmoid(b)
    p = r * gt
    z = np.sum(p, axis=1, keepdims=True)
    w = p * f64(size) / z
    wq = w * f64(qs)
    growsq = mxq(f64(grows), 0, "e4m3")
    wqq = mxq(wq, 0, "e4m3")
    gv = growsq.T @ wqq
    gf = np.zeros((E, T))
    gf[:, idx] = gv
    y = f64(old) * f64(fade) + gf
    return y

@@ -1,0 +1,182 @@
+from contextlib import ExitStack
+
+import concourse.mybir as mybir
+from concourse.masks import make_identity
+
+D, E, T, I, Q = 512, 512, 1024, 256, 512
+FLOPS = 2 * (2 * D * Q * I + Q * E * I)
+
+F32 = mybir.dt.float32
+BF16 = mybir.dt.bfloat16
+I32 = mybir.dt.int32
+U32 = mybir.dt.uint32
+U16 = mybir.dt.uint16
+U8 = mybir.dt.uint8
+FP8X4 = mybir.dt.float8_e4m3fn_x4
+ACT = mybir.ActivationFunctionType
+ALU = mybir.AluOpType
+
+P = 128
+PACK = 4
+BANK = 512
+HALF = 256
+
+
+def tile_attend_bgatedexp_b_v_kernel(tc, query, query2, keys_words, keys_scales, size, qs, grows, old, fade, offs, out):
+    nc = tc.nc
+    with ExitStack() as ctx:
+        sb = ctx.enter_context(tc.tile_pool(name="sb", bufs=1))
+        ps = ctx.enter_context(tc.psum_pool(name="ps", bufs=1))
+
+        def load_half(src, h, name):
+            raw = sb.tile([P, PACK, HALF], F32, name=name)
+            nc.sync.dma_start(raw[:], src.rearrange("(p j) w -> p j w", j=PACK)[:, :, h * HALF:(h + 1) * HALF])
+            return raw
+
+        b_banks = [ps.tile([P, BANK], F32, name="b_bank%d" % n) for n in range(2)]
+        a_banks = [ps.tile([P, BANK], F32, name="a_bank%d" % n) for n in range(4)]
+        row_bank = ps.tile([P, BANK], F32, name="row_bank")
+        spare_bank = ps.tile([P, BANK], F32, name="spare_bank")
+        pool_scales = sb.tile([P, T], U8, name="pool_scales", align_bytes=64)
+        offsets = sb.tile([P, I // 16], U16, name="offsets")
+        nc.sync.dma_start(offsets[:], offs)
+        pool_words = sb.tile([P, T], U32, name="pool_words", align_bytes=64)
+        nc.sync.dma_start(pool_words[:].bitcast(I32), keys_words[0].rearrange("p n t -> p (n t)").bitcast(I32))
+        for quad in range(4):
+            nc.scalar.dma_start(pool_scales[32 * quad:32 * quad + 32, :].bitcast(I32),
+                              keys_scales[0, 4 * quad:4 * quad + 4, :].bitcast(I32).partition_broadcast(8))
+        q2_raw = [load_half(query2, h, "q2_raw%d" % h) for h in range(2)]
+        q_raw = [load_half(query, h, "q_raw%d" % h) for h in range(2)]
+        size_pairs = sb.tile([P, 2], F32, name="size_pairs")
+        nc.sync.dma_start(size_pairs[:], size.rearrange("o (p u) -> p (o u)", u=2))
+        fade_rows = sb.tile([P, P], F32, name="fade_rows")
+        nc.gpsimd.memset(fade_rows[:], 0.0)
+        nc.sync.dma_start(fade_rows[0:T // P, :], fade.rearrange("o (k p) -> (o k) p", p=P))
+        qs_cols = sb.tile([P, PACK], F32, name="qs_cols")
+        nc.sync.dma_start(qs_cols[:], qs.rearrange("(p r) o -> p (r o)", r=PACK))
+        ident = sb.tile([P, P], F32, name="ident")
+        make_identity(nc, ident[:])
+        g_raw = [load_half(grows, h, "g_raw%d" % h) for h in range(2)]
+        old_raw = []
+        for j in range(4):
+            chunk = sb.tile([P, 4, HALF], F32, name="old_raw%d" % j)
+            nc.sync.dma_start(chunk[:], old.rearrange("(c p) t -> p c t", p=P)[:, :, j * HALF:(j + 1) * HALF])
+            old_raw.append(chunk)
+
+        windows = []
+        for c in range(4):
+            window = sb.tile([P, T], F32, name="window%d" % c)
+            (nc.vector if c < 2 else nc.gpsimd).memset(window[:], 0.0)
+            windows.append(window)
+
+        key_words = sb.tile([P, I], U32, name="key_words", align_bytes=64)
+        key_scales = sb.tile([P, I], U8, name="key_scales", align_bytes=64)
+        nc.vector.tensor_copy(key_words[:], pool_words[:].indirect(offsets[:]))
+        nc.vector.tensor_copy(key_scales[:], pool_scales[:].indirect(offsets[:]))
+
+        def scores(raw, name, outs):
+            dealt = sb.tile([P, PACK, P, PACK], BF16, name=name + "_dealt", align_bytes=64)
+            for h in range(2):
+                nc.vector.tensor_copy(
+                    dealt[:, :, h * 64:(h + 1) * 64, :].rearrange("p r s j -> p s j r"),
+                    raw[h][:].rearrange("p j (s r) -> p s j r", r=PACK))
+            for pair in range(2):
+                codes = sb.tile([P, 2 * P], U32, name="%s_codes%d" % (name, pair), align_bytes=64)
+                scales = sb.tile([P, 2 * P], U8, name="%s_scales%d" % (name, pair), align_bytes=64)
+                nc.vector.quantize_mx(codes[:].bitcast(FP8X4), scales[:],
+                                      dealt[:, 2 * pair:2 * pair + 2, :, :].rearrange("p r s j -> p (r s j)"))
+                for u in range(2):
+                    cols = slice(u * P, (u + 1) * P)
+                    nc.tensor.matmul_mx(outs[2 * pair + u], lhsT=codes[:, cols].bitcast(FP8X4), lhsT_scale=scales[:, cols],
+                                        rhs=key_words[:].bitcast(FP8X4), rhs_scale=key_scales[:], start=True, stop=True)
+
+        gates = []
+        scores(q2_raw, "b", [b_banks[r // 2][:, (r % 2) * I:(r % 2 + 1) * I] for r in range(PACK)])
+        for pair in range(2):
+            gate = sb.tile([P, 2 * I], F32, name="gate%d" % pair, align_bytes=64)
+            nc.scalar.activation(gate[:], b_banks[pair][:], ACT.Sigmoid)
+            gates.append(gate)
+
+        for u in range(2):
+            nc.tensor.transpose(b_banks[0][:, u * P:(u + 1) * P], size_pairs[:, u:u + 1].to_broadcast([P, P]), ident[:])
+        nc.tensor.transpose(b_banks[1][:, 0:P], fade_rows[:], ident[:])
+        fade_cols = sb.tile([P, T // P], F32, name="fade_cols")
+        nc.vector.tensor_copy(fade_cols[:], b_banks[1][:, 0:T // P])
+
+        scores(q_raw, "a", [a_banks[r][:, 0:I] for r in range(PACK)])
+        wq = sb.tile([P, PACK, I], F32, name="wq")
+        probs, row_sums = [], []
+        for pair in range(2):
+            row_sum = sb.tile([P, 2], F32, name="row_sum%d" % pair)
+            prob = sb.tile([P, 2, I], F32, name="prob%d" % pair)
+            for u in range(2):
+                score = a_banks[2 * pair + u][:, 0:I]
+                neg_max = sb.tile([P, 1], F32, name="neg_max%d" % (2 * pair + u))
+                nc.vector.tensor_reduce(neg_max[:], score, mybir.AxisListType.X, ALU.max, negate=True)
+                expo = sb.tile([P, I], F32, name="expo%d" % (2 * pair + u))
+                nc.scalar.activation(expo[:], score, ACT.Exp, bias=neg_max[:])
+                nc.vector.scalar_tensor_tensor(prob[:, u, :], expo[:], 1.0, gates[pair][:, u * I:(u + 1) * I], ALU.mult, ALU.mult,
+                                               accum_out=row_sum[:, u:u + 1])
+            probs.append(prob)
+            row_sums.append(row_sum)
+        for pair in range(2):
+            inv = sb.tile([P, 2], F32, name="inv%d" % pair)
+            nc.vector.reciprocal(inv[:], row_sums[pair][:])
+            row_factor = sb.tile([P, 2], F32, name="row_factor%d" % pair)
+            nc.vector.tensor_tensor(row_factor[:], inv[:], qs_cols[:, 2 * pair:2 * pair + 2], ALU.mult)
+            for u in range(2):
+                nc.vector.scalar_tensor_tensor(
+                    wq[:, 2 * pair + u, :].rearrange("p (n u) -> p n u", u=2),
+                    probs[pair][:, u, :].rearrange("p (n u) -> p n u", u=2),
+                    row_factor[:, u:u + 1], b_banks[0][:, 0:I].rearrange("p (u n) -> p n u", u=2), ALU.mult, ALU.mult)
+        wq_grouped = sb.tile([P, I, PACK], BF16, name="wq_grouped", align_bytes=64)
+        nc.vector.tensor_copy(wq_grouped[:].rearrange("p (c i) r -> p c r i", i=4),
+                              wq[:].rearrange("p r (c i) -> p c r i", i=4))
+        wq_codes = sb.tile([P, I], U32, name="wq_codes", align_bytes=64)
+        wq_scales = sb.tile([P, I], U8, name="wq_scales", align_bytes=64)
+        nc.vector.quantize_mx(wq_codes[:].bitcast(FP8X4), wq_scales[:], wq_grouped[:].rearrange("p i r -> p (i r)"))
+
+        g_quant = []
+        for h in range(2):
+            grouped = gates[h][:].bitcast(BF16)
+            nc.vector.tensor_copy(grouped.rearrange("p (c i j) -> p c j i", i=4, j=PACK),
+                                  g_raw[h][:].rearrange("p j (c i) -> p c j i", i=4))
+            codes = sb.tile([P, HALF], U32, name="g_codes%d" % h, align_bytes=64)
+            scales = sb.tile([P, HALF], U8, name="g_scales%d" % h, align_bytes=64)
+            nc.vector.quantize_mx(codes[:].bitcast(FP8X4), scales[:], grouped)
+            g_quant.append((codes, scales))
+
+        faded = []
+        for k in range(T // P):
+            bank = a_banks[k % 4]
+            for c in range(4):
+                nc.tensor.transpose(bank[:, c * P:(c + 1) * P], old_raw[k // 2][:, c, (k % 2) * P:(k % 2 + 1) * P], ident[:])
+            block = sb.tile([P, E], F32, name="faded%d" % k)
+            nc.scalar.activation(block[:], bank[:], ACT.Copy, scale=fade_cols[:, k:k + 1])
+            faded.append(block)
+
+        gv_psum = [row_bank[:, 0:I], b_banks[1][:, 0:I], spare_bank[:, 0:I], spare_bank[:, I:2 * I]]
+        for c in range(4):
+            codes, scales = g_quant[c // 2]
+            cols = slice((c % 2) * P, (c % 2 + 1) * P)
+            nc.tensor.matmul_mx(gv_psum[c], lhsT=codes[:, cols].bitcast(FP8X4), lhsT_scale=scales[:, cols],
+                                rhs=wq_codes[:].bitcast(FP8X4), rhs_scale=wq_scales[:], start=True, stop=True)
+        gv = [sb.tile([P, I], F32, name="gv%d" % c) for c in range(2)]
+        gv_late = sb.tile([P, 2 * I], F32, name="gv_late")
+        nc.scalar.copy(gv[0][:], gv_psum[0])
+        nc.scalar.activation(windows[0][:].indirect(offsets[:]), gv[0][:], ACT.Copy)
+        nc.vector.tensor_copy(gv[1][:], gv_psum[1])
+        nc.vector.tensor_copy(gv_late[:], spare_bank[:])
+        nc.vector.tensor_copy(windows[1][:].indirect(offsets[:]), gv[1][:])
+        for c in (2, 3):
+            nc.scalar.activation(windows[c][:].indirect(offsets[:]), gv_late[:, (c - 2) * I:(c - 1) * I], ACT.Copy)
+
+        back_banks = [b_banks[0], row_bank, b_banks[1], spare_bank]
+        for c in range(4):
+            for h in range(2):
+                bank = back_banks[(2 * c + h) % 4]
+                for kk in range(4):
+                    nc.tensor.transpose(bank[:, kk * P:(kk + 1) * P], faded[4 * h + kk][:, c * P:(c + 1) * P], ident[:])
+                result = sb.tile([P, BANK], F32, name="result%d_%d" % (c, h))
+                nc.vector.tensor_tensor(result[:], bank[:], windows[c][:, h * BANK:(h + 1) * BANK], ALU.add)
+                nc.sync.dma_start(out[c * P:(c + 1) * P, h * BANK:(h + 1) * BANK], result[:])

@@ -43,7 +43,7 @@ def tile_attend_bgatedexp_b_v_kernel(tc, query, query2, keys_words, keys_scales,
         pool_words = sb.tile([P, T], U32, name="pool_words", align_bytes=64)
         nc.sync.dma_start(pool_words[:].bitcast(I32), keys_words[0].rearrange("p n t -> p (n t)").bitcast(I32))
         for quad in range(4):
-            nc.scalar.dma_start(pool_scales[32 * quad:32 * quad + 32, :].bitcast(I32),
+            nc.sync.dma_start(pool_scales[32 * quad:32 * quad + 32, :].bitcast(I32),
                               keys_scales[0, 4 * quad:4 * quad + 4, :].bitcast(I32).partition_broadcast(8))
         q2_raw = [load_half(query2, h, "q2_raw%d" % h) for h in range(2)]
         q_raw = [load_half(query, h, "q_raw%d" % h) for h in range(2)]
@@ -74,8 +74,9 @@ def tile_attend_bgatedexp_b_v_kernel(tc, query, query2, keys_words, keys_scales,
         nc.vector.tensor_copy(key_words[:], pool_words[:].indirect(offsets[:]))
         nc.vector.tensor_copy(key_scales[:], pool_scales[:].indirect(offsets[:]))
 
+        dealt = sb.tile([P, PACK, P, PACK], BF16, name="dealt", align_bytes=64)
+
         def scores(raw, name, outs):
-            dealt = sb.tile([P, PACK, P, PACK], BF16, name=name + "_dealt", align_bytes=64)
             for h in range(2):
                 nc.vector.tensor_copy(
                     dealt[:, :, h * 64:(h + 1) * 64, :].rearrange("p r s j -> p s j r"),
@@ -99,24 +100,24 @@ def tile_attend_bgatedexp_b_v_kernel(tc, query, query2, keys_words, keys_scales,
 
         for u in range(2):
             nc.tensor.transpose(b_banks[0][:, u * P:(u + 1) * P], size_pairs[:, u:u + 1].to_broadcast([P, P]), ident[:])
-        nc.tensor.transpose(b_banks[1][:, 0:P], fade_rows[:], ident[:])
-        fade_cols = sb.tile([P, T // P], F32, name="fade_cols")
-        nc.vector.tensor_copy(fade_cols[:], b_banks[1][:, 0:T // P])
 
+        nc.tensor.transpose(b_banks[1][:, 0:P], fade_rows[:], ident[:])
         scores(q_raw, "a", [a_banks[r][:, 0:I] for r in range(PACK)])
         wq = sb.tile([P, PACK, I], F32, name="wq")
+        fade_cols = sb.tile([P, T // P], F32, name="fade_cols")
+        neg_max = [sb.tile([P, 1], F32, name="neg_max%d" % r) for r in range(PACK - 1)] + [fade_cols[:, 0:1]]
+        expo = [sb.tile([P, I], F32, name="expo%d" % r) for r in range(PACK)]
+        for r in range(PACK):
+            nc.vector.tensor_reduce(neg_max[r][:], a_banks[r][:, 0:I], mybir.AxisListType.X, ALU.max, negate=True)
+            nc.scalar.activation(expo[r][:], a_banks[r][:, 0:I], ACT.Exp, bias=neg_max[r][:])
+        nc.scalar.copy(fade_cols[:], b_banks[1][:, 0:T // P])
         probs, row_sums = [], []
         for pair in range(2):
             row_sum = sb.tile([P, 2], F32, name="row_sum%d" % pair)
             prob = sb.tile([P, 2, I], F32, name="prob%d" % pair)
             for u in range(2):
-                score = a_banks[2 * pair + u][:, 0:I]
-                neg_max = sb.tile([P, 1], F32, name="neg_max%d" % (2 * pair + u))
-                nc.vector.tensor_reduce(neg_max[:], score, mybir.AxisListType.X, ALU.max, negate=True)
-                expo = sb.tile([P, I], F32, name="expo%d" % (2 * pair + u))
-                nc.scalar.activation(expo[:], score, ACT.Exp, bias=neg_max[:])
-                nc.vector.scalar_tensor_tensor(prob[:, u, :], expo[:], 1.0, gates[pair][:, u * I:(u + 1) * I], ALU.mult, ALU.mult,
-                                               accum_out=row_sum[:, u:u + 1])
+                nc.vector.scalar_tensor_tensor(prob[:, u, :], expo[2 * pair + u][:], 1.0, gates[pair][:, u * I:(u + 1) * I],
+                                               ALU.mult, ALU.mult, accum_out=row_sum[:, u:u + 1])
             probs.append(prob)
             row_sums.append(row_sum)
         for pair in range(2):
@@ -129,22 +130,22 @@ def tile_attend_bgatedexp_b_v_kernel(tc, query, query2, keys_words, keys_scales,
                     wq[:, 2 * pair + u, :].rearrange("p (n u) -> p n u", u=2),
                     probs[pair][:, u, :].rearrange("p (n u) -> p n u", u=2),
                     row_factor[:, u:u + 1], b_banks[0][:, 0:I].rearrange("p (u n) -> p n u", u=2), ALU.mult, ALU.mult)
-        wq_grouped = sb.tile([P, I, PACK], BF16, name="wq_grouped", align_bytes=64)
-        nc.vector.tensor_copy(wq_grouped[:].rearrange("p (c i) r -> p c r i", i=4),
-                              wq[:].rearrange("p r (c i) -> p c r i", i=4))
-        wq_codes = sb.tile([P, I], U32, name="wq_codes", align_bytes=64)
-        wq_scales = sb.tile([P, I], U8, name="wq_scales", align_bytes=64)
-        nc.vector.quantize_mx(wq_codes[:].bitcast(FP8X4), wq_scales[:], wq_grouped[:].rearrange("p i r -> p (i r)"))
-
         g_quant = []
         for h in range(2):
-            grouped = gates[h][:].bitcast(BF16)
+            grouped = dealt[:, 2:4].rearrange("p r s j -> p (r s j)") if h == 0 else gates[1][:].bitcast(BF16)
             nc.vector.tensor_copy(grouped.rearrange("p (c i j) -> p c j i", i=4, j=PACK),
                                   g_raw[h][:].rearrange("p j (c i) -> p c j i", i=4))
             codes = sb.tile([P, HALF], U32, name="g_codes%d" % h, align_bytes=64)
             scales = sb.tile([P, HALF], U8, name="g_scales%d" % h, align_bytes=64)
             nc.vector.quantize_mx(codes[:].bitcast(FP8X4), scales[:], grouped)
             g_quant.append((codes, scales))
+
+        wq_grouped = sb.tile([P, I, PACK], BF16, name="wq_grouped", align_bytes=64)
+        nc.vector.tensor_copy(wq_grouped[:].rearrange("p (c i) r -> p c r i", i=4),
+                              wq[:].rearrange("p r (c i) -> p c r i", i=4))
+        wq_codes = sb.tile([P, I], U32, name="wq_codes", align_bytes=64)
+        wq_scales = sb.tile([P, I], U8, name="wq_scales", align_bytes=64)
+        nc.vector.quantize_mx(wq_codes[:].bitcast(FP8X4), wq_scales[:], wq_grouped[:].rearrange("p i r -> p (i r)"))
 
         faded = []
         for k in range(T // P):
@@ -155,23 +156,20 @@ def tile_attend_bgatedexp_b_v_kernel(tc, query, query2, keys_words, keys_scales,
             nc.scalar.activation(block[:], bank[:], ACT.Copy, scale=fade_cols[:, k:k + 1])
             faded.append(block)
 
-        gv_psum = [row_bank[:, 0:I], b_banks[1][:, 0:I], spare_bank[:, 0:I], spare_bank[:, I:2 * I]]
+        back_banks = [row_bank, b_banks[1], spare_bank, b_banks[0]]
+        gv_psum = [bank[:, 0:I] for bank in back_banks]
         for c in range(4):
             codes, scales = g_quant[c // 2]
             cols = slice((c % 2) * P, (c % 2 + 1) * P)
             nc.tensor.matmul_mx(gv_psum[c], lhsT=codes[:, cols].bitcast(FP8X4), lhsT_scale=scales[:, cols],
                                 rhs=wq_codes[:].bitcast(FP8X4), rhs_scale=wq_scales[:], start=True, stop=True)
-        gv = [sb.tile([P, I], F32, name="gv%d" % c) for c in range(2)]
-        gv_late = sb.tile([P, 2 * I], F32, name="gv_late")
-        nc.scalar.copy(gv[0][:], gv_psum[0])
-        nc.scalar.activation(windows[0][:].indirect(offsets[:]), gv[0][:], ACT.Copy)
-        nc.vector.tensor_copy(gv[1][:], gv_psum[1])
-        nc.vector.tensor_copy(gv_late[:], spare_bank[:])
+        gv = [sb.tile([P, I], F32, name="gv%d" % c) for c in range(4)]
+        for c in range(4):
+            nc.vector.tensor_copy(gv[c][:], gv_psum[c])
         nc.vector.tensor_copy(windows[1][:].indirect(offsets[:]), gv[1][:])
-        for c in (2, 3):
-            nc.scalar.activation(windows[c][:].indirect(offsets[:]), gv_late[:, (c - 2) * I:(c - 1) * I], ACT.Copy)
+        for c in (0, 2, 3):
+            nc.scalar.activation(windows[c][:].indirect(offsets[:]), gv[c][:], ACT.Copy)
 
-        back_banks = [b_banks[0], row_bank, b_banks[1], spare_bank]
         for c in range(4):
             for h in range(2):
                 bank = back_banks[(2 * c + h) % 4]

@@ -40,6 +40,8 @@ def tile_attend_bgatedexp_b_v_kernel(tc, query, query2, keys_words, keys_scales,
         pool_scales = sb.tile([P, T], U8, name="pool_scales", align_bytes=64)
         offsets = sb.tile([P, I // 16], U16, name="offsets")
         nc.sync.dma_start(offsets[:], offs)
+        fade_runs = sb.tile([P, 8], F32, name="fade_runs")
+        nc.sync.dma_start(fade_runs[:], fade.rearrange("o (p u) -> p (o u)", u=8))
         pool_words = sb.tile([P, T], U32, name="pool_words", align_bytes=64)
         nc.sync.dma_start(pool_words[:].bitcast(I32), keys_words[0].rearrange("p n t -> p (n t)").bitcast(I32))
         for quad in range(4):
@@ -59,9 +61,11 @@ def tile_attend_bgatedexp_b_v_kernel(tc, query, query2, keys_words, keys_scales,
         g_raw = [load_half(grows, h, "g_raw%d" % h) for h in range(2)]
         old_raw = []
         for j in range(4):
-            chunk = sb.tile([P, 4, HALF], F32, name="old_raw%d" % j)
-            nc.sync.dma_start(chunk[:], old.rearrange("(c p) t -> p c t", p=P)[:, :, j * HALF:(j + 1) * HALF])
+            chunk = sb.tile([P, 4, HALF], F32, name="old_raw%d" % j, align_bytes=64)
+            nc.sync.dma_start(chunk[:, 0:3], old.rearrange("(c p) t -> p c t", p=P)[:, 1:4, j * HALF:(j + 1) * HALF])
             old_raw.append(chunk)
+        old_first = sb.tile([P, T], F32, name="old_first")
+        nc.sync.dma_start(old_first[:], old[0:P, :])
 
         windows = []
         for c in range(4):
@@ -69,6 +73,13 @@ def tile_attend_bgatedexp_b_v_kernel(tc, query, query2, keys_words, keys_scales,
             (nc.vector if c < 2 else nc.gpsimd).memset(window[:], 0.0)
             windows.append(window)
 
+        fade_wide = sb.tile([P, T], F32, name="fade_wide")
+        for h in range(2):
+            for u in range(4):
+                nc.tensor.transpose(a_banks[h][:, u * P:(u + 1) * P],
+                                    fade_runs[:, 4 * h + u:4 * h + u + 1].to_broadcast([P, P]), ident[:])
+            nc.scalar.copy(fade_wide[:].rearrange("p (n h u) -> p h n u", h=2, u=4)[:, h],
+                           a_banks[h][:].rearrange("p (u n) -> p n u", u=4))
         key_words = sb.tile([P, I], U32, name="key_words", align_bytes=64)
         key_scales = sb.tile([P, I], U8, name="key_scales", align_bytes=64)
         nc.vector.tensor_copy(key_words[:], pool_words[:].indirect(offsets[:]))
@@ -104,13 +115,14 @@ def tile_attend_bgatedexp_b_v_kernel(tc, query, query2, keys_words, keys_scales,
         nc.tensor.transpose(b_banks[1][:, 0:P], fade_rows[:], ident[:])
         scores(q_raw, "a", [a_banks[r][:, 0:I] for r in range(PACK)])
         wq = sb.tile([P, PACK, I], F32, name="wq")
-        fade_cols = sb.tile([P, T // P], F32, name="fade_cols")
+        gv = [sb.tile([P, I], F32, name="gv%d" % c) for c in range(4)]
+        fade_cols = gv[0][:, 0:T // P]
         neg_max = [sb.tile([P, 1], F32, name="neg_max%d" % r) for r in range(PACK - 1)] + [fade_cols[:, 0:1]]
         expo = [sb.tile([P, I], F32, name="expo%d" % r) for r in range(PACK)]
         for r in range(PACK):
             nc.vector.tensor_reduce(neg_max[r][:], a_banks[r][:, 0:I], mybir.AxisListType.X, ALU.max, negate=True)
             nc.scalar.activation(expo[r][:], a_banks[r][:, 0:I], ACT.Exp, bias=neg_max[r][:])
-        nc.scalar.copy(fade_cols[:], b_banks[1][:, 0:T // P])
+        nc.scalar.copy(fade_cols, b_banks[1][:, 0:T // P])
         probs, row_sums = [], []
         for pair in range(2):
             row_sum = sb.tile([P, 2], F32, name="row_sum%d" % pair)
@@ -130,31 +142,33 @@ def tile_attend_bgatedexp_b_v_kernel(tc, query, query2, keys_words, keys_scales,
                     wq[:, 2 * pair + u, :].rearrange("p (n u) -> p n u", u=2),
                     probs[pair][:, u, :].rearrange("p (n u) -> p n u", u=2),
                     row_factor[:, u:u + 1], b_banks[0][:, 0:I].rearrange("p (u n) -> p n u", u=2), ALU.mult, ALU.mult)
-        g_quant = []
-        for h in range(2):
-            grouped = dealt[:, 2:4].rearrange("p r s j -> p (r s j)") if h == 0 else gates[1][:].bitcast(BF16)
+        def quantise_grows(h, grouped):
             nc.vector.tensor_copy(grouped.rearrange("p (c i j) -> p c j i", i=4, j=PACK),
                                   g_raw[h][:].rearrange("p j (c i) -> p c j i", i=4))
             codes = sb.tile([P, HALF], U32, name="g_codes%d" % h, align_bytes=64)
             scales = sb.tile([P, HALF], U8, name="g_scales%d" % h, align_bytes=64)
             nc.vector.quantize_mx(codes[:].bitcast(FP8X4), scales[:], grouped)
-            g_quant.append((codes, scales))
+            return codes, scales
 
-        wq_grouped = sb.tile([P, I, PACK], BF16, name="wq_grouped", align_bytes=64)
+        g_quant = [quantise_grows(0, dealt[:, 2:4].rearrange("p r s j -> p (r s j)"))]
+        faded = []
+        for k in range(T // P):
+            bank = a_banks[k % 4]
+            for c in range(3):
+                nc.tensor.transpose(bank[:, c * P:(c + 1) * P], old_raw[k // 2][:, c, (k % 2) * P:(k % 2 + 1) * P], ident[:])
+            block = sb.tile([P, 3 * P], F32, name="faded%d" % k)
+            nc.scalar.activation(block[:], bank[:, 0:3 * P], ACT.Copy, scale=fade_cols[:, k:k + 1])
+            faded.append(block)
+
+        stage = old_raw[3][:].rearrange("p c t -> p (c t)")
+        wq_grouped = stage[:, BANK:T].bitcast(BF16).rearrange("p (i r) -> p i r", r=PACK)
         nc.vector.tensor_copy(wq_grouped[:].rearrange("p (c i) r -> p c r i", i=4),
                               wq[:].rearrange("p r (c i) -> p c r i", i=4))
         wq_codes = sb.tile([P, I], U32, name="wq_codes", align_bytes=64)
         wq_scales = sb.tile([P, I], U8, name="wq_scales", align_bytes=64)
         nc.vector.quantize_mx(wq_codes[:].bitcast(FP8X4), wq_scales[:], wq_grouped[:].rearrange("p i r -> p (i r)"))
 
-        faded = []
-        for k in range(T // P):
-            bank = a_banks[k % 4]
-            for c in range(4):
-                nc.tensor.transpose(bank[:, c * P:(c + 1) * P], old_raw[k // 2][:, c, (k % 2) * P:(k % 2 + 1) * P], ident[:])
-            block = sb.tile([P, E], F32, name="faded%d" % k)
-            nc.scalar.activation(block[:], bank[:], ACT.Copy, scale=fade_cols[:, k:k + 1])
-            faded.append(block)
+        g_quant.append(quantise_grows(1, wq_grouped[:].rearrange("p i r -> p (i r)")))
 
         back_banks = [row_bank, b_banks[1], spare_bank, b_banks[0]]
         gv_psum = [bank[:, 0:I] for bank in back_banks]
@@ -163,18 +177,25 @@ def tile_attend_bgatedexp_b_v_kernel(tc, query, query2, keys_words, keys_scales,
             cols = slice((c % 2) * P, (c % 2 + 1) * P)
             nc.tensor.matmul_mx(gv_psum[c], lhsT=codes[:, cols].bitcast(FP8X4), lhsT_scale=scales[:, cols],
                                 rhs=wq_codes[:].bitcast(FP8X4), rhs_scale=wq_scales[:], start=True, stop=True)
-        gv = [sb.tile([P, I], F32, name="gv%d" % c) for c in range(4)]
         for c in range(4):
-            nc.vector.tensor_copy(gv[c][:], gv_psum[c])
-        nc.vector.tensor_copy(windows[1][:].indirect(offsets[:]), gv[1][:])
-        for c in (0, 2, 3):
-            nc.scalar.activation(windows[c][:].indirect(offsets[:]), gv[c][:], ACT.Copy)
+            (nc.scalar.copy if c % 2 == 0 else nc.vector.tensor_copy)(gv[c][:], gv_psum[c])
+            if c == 1:
+                nc.vector.tensor_copy(windows[c][:].indirect(offsets[:]), gv[c][:])
+            else:
+                nc.scalar.activation(windows[c][:].indirect(offsets[:]), gv[c][:], ACT.Copy)
 
-        for c in range(4):
+        for c in range(1, 4):
             for h in range(2):
-                bank = back_banks[(2 * c + h) % 4]
+                bank = back_banks[(2 * (c - 1) + h) % 4]
                 for kk in range(4):
-                    nc.tensor.transpose(bank[:, kk * P:(kk + 1) * P], faded[4 * h + kk][:, c * P:(c + 1) * P], ident[:])
+                    nc.tensor.transpose(bank[:, kk * P:(kk + 1) * P], faded[4 * h + kk][:, (c - 1) * P:c * P], ident[:])
                 result = sb.tile([P, BANK], F32, name="result%d_%d" % (c, h))
                 nc.vector.tensor_tensor(result[:], bank[:], windows[c][:, h * BANK:(h + 1) * BANK], ALU.add)
                 nc.sync.dma_start(out[c * P:(c + 1) * P, h * BANK:(h + 1) * BANK], result[:])
+
+        nc.gpsimd.tensor_tensor(stage, old_first[:], fade_wide[:], ALU.mult)
+        for h in range(2):
+            cols = slice(h * BANK, (h + 1) * BANK)
+            result = sb.tile([P, BANK], F32, name="result0_%d" % h)
+            nc.gpsimd.tensor_tensor(result[:], stage[:, cols], windows[0][:, cols], ALU.add)
+            nc.sync.dma_start(out[0:P, cols], result[:])

@@ -142,15 +142,15 @@ def tile_attend_bgatedexp_b_v_kernel(tc, query, query2, keys_words, keys_scales,
                     wq[:, 2 * pair + u, :].rearrange("p (n u) -> p n u", u=2),
                     probs[pair][:, u, :].rearrange("p (n u) -> p n u", u=2),
                     row_factor[:, u:u + 1], b_banks[0][:, 0:I].rearrange("p (u n) -> p n u", u=2), ALU.mult, ALU.mult)
-        def quantise_grows(h, grouped):
-            nc.vector.tensor_copy(grouped.rearrange("p (c i j) -> p c j i", i=4, j=PACK),
-                                  g_raw[h][:].rearrange("p j (c i) -> p c j i", i=4))
+        def quantise_grows(h, grouped, copy):
+            copy(grouped.rearrange("p (c i j) -> p c j i", i=4, j=PACK),
+                 g_raw[h][:].rearrange("p j (c i) -> p c j i", i=4))
             codes = sb.tile([P, HALF], U32, name="g_codes%d" % h, align_bytes=64)
             scales = sb.tile([P, HALF], U8, name="g_scales%d" % h, align_bytes=64)
             nc.vector.quantize_mx(codes[:].bitcast(FP8X4), scales[:], grouped)
             return codes, scales
 
-        g_quant = [quantise_grows(0, dealt[:, 2:4].rearrange("p r s j -> p (r s j)"))]
+        g_quant = [quantise_grows(0, dealt[:, 2:4].rearrange("p r s j -> p (r s j)"), nc.vector.tensor_copy)]
         faded = []
         for k in range(T // P):
             bank = a_banks[k % 4]
@@ -168,7 +168,7 @@ def tile_attend_bgatedexp_b_v_kernel(tc, query, query2, keys_words, keys_scales,
         wq_scales = sb.tile([P, I], U8, name="wq_scales", align_bytes=64)
         nc.vector.quantize_mx(wq_codes[:].bitcast(FP8X4), wq_scales[:], wq_grouped[:].rearrange("p i r -> p (i r)"))
 
-        g_quant.append(quantise_grows(1, wq_grouped[:].rearrange("p i r -> p (i r)")))
+        g_quant.append(quantise_grows(1, stage[:, 0:BANK].bitcast(BF16), nc.scalar.copy))
 
         back_banks = [row_bank, b_banks[1], spare_bank, b_banks[0]]
         gv_psum = [bank[:, 0:I] for bank in back_banks]
@@ -178,15 +178,15 @@ def tile_attend_bgatedexp_b_v_kernel(tc, query, query2, keys_words, keys_scales,
             nc.tensor.matmul_mx(gv_psum[c], lhsT=codes[:, cols].bitcast(FP8X4), lhsT_scale=scales[:, cols],
                                 rhs=wq_codes[:].bitcast(FP8X4), rhs_scale=wq_scales[:], start=True, stop=True)
         for c in range(4):
-            (nc.scalar.copy if c % 2 == 0 else nc.vector.tensor_copy)(gv[c][:], gv_psum[c])
-            if c == 1:
+            (nc.scalar.copy if c == 0 else nc.vector.tensor_copy)(gv[c][:], gv_psum[c])
+            if c == 3:
                 nc.vector.tensor_copy(windows[c][:].indirect(offsets[:]), gv[c][:])
             else:
                 nc.scalar.activation(windows[c][:].indirect(offsets[:]), gv[c][:], ACT.Copy)
 
-        for c in range(1, 4):
+        for n, c in enumerate((3, 1, 2)):
             for h in range(2):
-                bank = back_banks[(2 * (c - 1) + h) % 4]
+                bank = back_banks[(2 * n + h) % 4]
                 for kk in range(4):
                     nc.tensor.transpose(bank[:, kk * P:(kk + 1) * P], faded[4 * h + kk][:, (c - 1) * P:c * P], ident[:])
                 result = sb.tile([P, BANK], F32, name="result%d_%d" % (c, h))

@@ -20,6 +20,10 @@ P = 128
 PACK = 4
 BANK = 512
 HALF = 256
+TILES = E // P
+TURNED = TILES - 1
+BLOCKS = T // P
+LINE = 4
 
 
 def tile_attend_bgatedexp_b_v_kernel(tc, query, query2, keys_words, keys_scales, size, qs, grows, old, fade, offs, out):
@@ -34,14 +38,14 @@ def tile_attend_bgatedexp_b_v_kernel(tc, query, query2, keys_words, keys_scales,
             return raw
 
         b_banks = [ps.tile([P, BANK], F32, name="b_bank%d" % n) for n in range(2)]
-        a_banks = [ps.tile([P, BANK], F32, name="a_bank%d" % n) for n in range(4)]
-        row_bank = ps.tile([P, BANK], F32, name="row_bank")
-        spare_bank = ps.tile([P, BANK], F32, name="spare_bank")
+        a_banks = [ps.tile([P, BANK], F32, name="a_bank%d" % n) for n in range(PACK)]
+        gv_banks = [ps.tile([P, BANK], F32, name="gv_bank%d" % n) for n in range(2)]
+
         pool_scales = sb.tile([P, T], U8, name="pool_scales", align_bytes=64)
         offsets = sb.tile([P, I // 16], U16, name="offsets")
         nc.sync.dma_start(offsets[:], offs)
-        fade_runs = sb.tile([P, 8], F32, name="fade_runs")
-        nc.sync.dma_start(fade_runs[:], fade.rearrange("o (p u) -> p (o u)", u=8))
+        fade_runs = sb.tile([P, BLOCKS], F32, name="fade_runs")
+        nc.sync.dma_start(fade_runs[:], fade.rearrange("o (p u) -> p (o u)", u=BLOCKS))
         pool_words = sb.tile([P, T], U32, name="pool_words", align_bytes=64)
         nc.sync.dma_start(pool_words[:].bitcast(I32), keys_words[0].rearrange("p n t -> p (n t)").bitcast(I32))
         for quad in range(4):
@@ -53,24 +57,25 @@ def tile_attend_bgatedexp_b_v_kernel(tc, query, query2, keys_words, keys_scales,
         nc.sync.dma_start(size_pairs[:], size.rearrange("o (p u) -> p (o u)", u=2))
         fade_rows = sb.tile([P, P], F32, name="fade_rows")
         nc.gpsimd.memset(fade_rows[:], 0.0)
-        nc.sync.dma_start(fade_rows[0:T // P, :], fade.rearrange("o (k p) -> (o k) p", p=P))
+        nc.sync.dma_start(fade_rows[0:BLOCKS, :], fade.rearrange("o (k p) -> (o k) p", p=P))
         qs_cols = sb.tile([P, PACK], F32, name="qs_cols")
         nc.sync.dma_start(qs_cols[:], qs.rearrange("(p r) o -> p (r o)", r=PACK))
         ident = sb.tile([P, P], F32, name="ident")
         make_identity(nc, ident[:])
         g_raw = [load_half(grows, h, "g_raw%d" % h) for h in range(2)]
         old_raw = []
-        for j in range(4):
-            chunk = sb.tile([P, 4, HALF], F32, name="old_raw%d" % j, align_bytes=64)
-            nc.sync.dma_start(chunk[:, 0:3], old.rearrange("(c p) t -> p c t", p=P)[:, 1:4, j * HALF:(j + 1) * HALF])
+        for j in range(T // HALF):
+            chunk = sb.tile([P, TILES, HALF], F32, name="old_raw%d" % j, align_bytes=64)
+            nc.sync.dma_start(chunk[:, 0:TURNED],
+                              old.rearrange("(c p) t -> p c t", p=P)[:, 1:TILES, j * HALF:(j + 1) * HALF])
             old_raw.append(chunk)
         old_first = sb.tile([P, T], F32, name="old_first")
         nc.sync.dma_start(old_first[:], old[0:P, :])
 
         windows = []
-        for c in range(4):
+        for c in range(TILES):
             window = sb.tile([P, T], F32, name="window%d" % c)
-            (nc.vector if c < 2 else nc.gpsimd).memset(window[:], 0.0)
+            (nc.vector if c < TILES // 2 else nc.gpsimd).memset(window[:], 0.0)
             windows.append(window)
 
         fade_wide = sb.tile([P, T], F32, name="fade_wide")
@@ -80,6 +85,7 @@ def tile_attend_bgatedexp_b_v_kernel(tc, query, query2, keys_words, keys_scales,
                                     fade_runs[:, 4 * h + u:4 * h + u + 1].to_broadcast([P, P]), ident[:])
             nc.scalar.copy(fade_wide[:].rearrange("p (n h u) -> p h n u", h=2, u=4)[:, h],
                            a_banks[h][:].rearrange("p (u n) -> p n u", u=4))
+
         key_words = sb.tile([P, I], U32, name="key_words", align_bytes=64)
         key_scales = sb.tile([P, I], U8, name="key_scales", align_bytes=64)
         nc.vector.tensor_copy(key_words[:], pool_words[:].indirect(offsets[:]))
@@ -88,9 +94,10 @@ def tile_attend_bgatedexp_b_v_kernel(tc, query, query2, keys_words, keys_scales,
         dealt = sb.tile([P, PACK, P, PACK], BF16, name="dealt", align_bytes=64)
 
         def scores(raw, name, outs):
+            rows = HALF // PACK
             for h in range(2):
                 nc.vector.tensor_copy(
-                    dealt[:, :, h * 64:(h + 1) * 64, :].rearrange("p r s j -> p s j r"),
+                    dealt[:, :, h * rows:(h + 1) * rows, :].rearrange("p r s j -> p s j r"),
                     raw[h][:].rearrange("p j (s r) -> p s j r", r=PACK))
             for pair in range(2):
                 codes = sb.tile([P, 2 * P], U32, name="%s_codes%d" % (name, pair), align_bytes=64)
@@ -111,18 +118,19 @@ def tile_attend_bgatedexp_b_v_kernel(tc, query, query2, keys_words, keys_scales,
 
         for u in range(2):
             nc.tensor.transpose(b_banks[0][:, u * P:(u + 1) * P], size_pairs[:, u:u + 1].to_broadcast([P, P]), ident[:])
-
         nc.tensor.transpose(b_banks[1][:, 0:P], fade_rows[:], ident[:])
+
         scores(q_raw, "a", [a_banks[r][:, 0:I] for r in range(PACK)])
         wq = sb.tile([P, PACK, I], F32, name="wq")
-        gv = [sb.tile([P, I], F32, name="gv%d" % c) for c in range(4)]
-        fade_cols = gv[0][:, 0:T // P]
-        neg_max = [sb.tile([P, 1], F32, name="neg_max%d" % r) for r in range(PACK - 1)] + [fade_cols[:, 0:1]]
+        gv_all = sb.tile([P, TILES * I], F32, name="gv_all")
+        gv = [gv_all[:, c * I:(c + 1) * I] for c in range(TILES)]
+        neg_max = [sb.tile([P, 1], F32, name="neg_max%d" % r) for r in range(PACK - 1)] + [gv_all[:, 0:1]]
         expo = [sb.tile([P, I], F32, name="expo%d" % r) for r in range(PACK)]
         for r in range(PACK):
             nc.vector.tensor_reduce(neg_max[r][:], a_banks[r][:, 0:I], mybir.AxisListType.X, ALU.max, negate=True)
             nc.scalar.activation(expo[r][:], a_banks[r][:, 0:I], ACT.Exp, bias=neg_max[r][:])
-        nc.scalar.copy(fade_cols, b_banks[1][:, 0:T // P])
+        nc.scalar.copy(gv_all[:].rearrange("p (c i) -> p c i", c=TILES)[:, :, 0:BLOCKS // TILES],
+                       b_banks[1][:, 0:BLOCKS].rearrange("p (j c) -> p c j", c=TILES))
         probs, row_sums = [], []
         for pair in range(2):
             row_sum = sb.tile([P, 2], F32, name="row_sum%d" % pair)
@@ -142,60 +150,67 @@ def tile_attend_bgatedexp_b_v_kernel(tc, query, query2, keys_words, keys_scales,
                     wq[:, 2 * pair + u, :].rearrange("p (n u) -> p n u", u=2),
                     probs[pair][:, u, :].rearrange("p (n u) -> p n u", u=2),
                     row_factor[:, u:u + 1], b_banks[0][:, 0:I].rearrange("p (u n) -> p n u", u=2), ALU.mult, ALU.mult)
+
         def quantise_grows(h, grouped, copy):
-            copy(grouped.rearrange("p (c i j) -> p c j i", i=4, j=PACK),
-                 g_raw[h][:].rearrange("p j (c i) -> p c j i", i=4))
+            copy(grouped.rearrange("p (c i j) -> p c j i", i=LINE, j=PACK),
+                 g_raw[h][:].rearrange("p j (c i) -> p c j i", i=LINE))
             codes = sb.tile([P, HALF], U32, name="g_codes%d" % h, align_bytes=64)
             scales = sb.tile([P, HALF], U8, name="g_scales%d" % h, align_bytes=64)
             nc.vector.quantize_mx(codes[:].bitcast(FP8X4), scales[:], grouped)
             return codes, scales
 
         g_quant = [quantise_grows(0, dealt[:, 2:4].rearrange("p r s j -> p (r s j)"), nc.vector.tensor_copy)]
+
         faded = []
-        for k in range(T // P):
-            bank = a_banks[k % 4]
-            for c in range(3):
+        for k in range(BLOCKS):
+            bank = a_banks[k % len(a_banks)]
+            for c in range(TURNED):
                 nc.tensor.transpose(bank[:, c * P:(c + 1) * P], old_raw[k // 2][:, c, (k % 2) * P:(k % 2 + 1) * P], ident[:])
-            block = sb.tile([P, 3 * P], F32, name="faded%d" % k)
-            nc.scalar.activation(block[:], bank[:, 0:3 * P], ACT.Copy, scale=fade_cols[:, k:k + 1])
+            block = sb.tile([P, TURNED * P], F32, name="faded%d" % k)
+            fade_col = gv[k % TILES][:, k // TILES:k // TILES + 1]
+            nc.scalar.activation(block[:], bank[:, 0:TURNED * P], ACT.Copy, scale=fade_col)
             faded.append(block)
 
-        stage = old_raw[3][:].rearrange("p c t -> p (c t)")
+        stage = old_raw[-1][:].rearrange("p c t -> p (c t)")
         wq_grouped = stage[:, BANK:T].bitcast(BF16).rearrange("p (i r) -> p i r", r=PACK)
-        nc.vector.tensor_copy(wq_grouped[:].rearrange("p (c i) r -> p c r i", i=4),
-                              wq[:].rearrange("p r (c i) -> p c r i", i=4))
+        nc.vector.tensor_copy(wq_grouped[:].rearrange("p (c i) r -> p c r i", i=LINE),
+                              wq[:].rearrange("p r (c i) -> p c r i", i=LINE))
         wq_codes = sb.tile([P, I], U32, name="wq_codes", align_bytes=64)
         wq_scales = sb.tile([P, I], U8, name="wq_scales", align_bytes=64)
         nc.vector.quantize_mx(wq_codes[:].bitcast(FP8X4), wq_scales[:], wq_grouped[:].rearrange("p i r -> p (i r)"))
-
         g_quant.append(quantise_grows(1, stage[:, 0:BANK].bitcast(BF16), nc.scalar.copy))
 
-        back_banks = [row_bank, b_banks[1], spare_bank, b_banks[0]]
-        gv_psum = [bank[:, 0:I] for bank in back_banks]
-        for c in range(4):
+        late_banks = [gv_banks[0], b_banks[1], gv_banks[1], b_banks[0]]
+        gv_psum = [bank[:, 0:I] for bank in late_banks]
+        for c in range(TILES):
             codes, scales = g_quant[c // 2]
             cols = slice((c % 2) * P, (c % 2 + 1) * P)
             nc.tensor.matmul_mx(gv_psum[c], lhsT=codes[:, cols].bitcast(FP8X4), lhsT_scale=scales[:, cols],
                                 rhs=wq_codes[:].bitcast(FP8X4), rhs_scale=wq_scales[:], start=True, stop=True)
-        for c in range(4):
-            (nc.scalar.copy if c == 0 else nc.vector.tensor_copy)(gv[c][:], gv_psum[c])
-            if c == 3:
-                nc.vector.tensor_copy(windows[c][:].indirect(offsets[:]), gv[c][:])
+        for c in range(TILES):
+            nc.vector.tensor_copy(gv[c], gv_psum[c])
+            if c == TILES - 1:
+                nc.vector.tensor_copy(windows[c][:].indirect(offsets[:]), gv[c])
             else:
-                nc.scalar.activation(windows[c][:].indirect(offsets[:]), gv[c][:], ACT.Copy)
+                nc.scalar.activation(windows[c][:].indirect(offsets[:]), gv[c], ACT.Copy)
+
+        shared = sb.tile([P, 2, BANK], F32, name="shared")
+        first_half = sb.tile([P, BANK], F32, name="first_half")
+        nc.gpsimd.tensor_tensor(stage, old_first[:], fade_wide[:], ALU.mult)
+        nc.gpsimd.tensor_tensor(first_half[:], stage[:, 0:BANK], windows[0][:, 0:BANK], ALU.add)
+        nc.sync.dma_start(out[0:P, 0:BANK], first_half[:])
+        nc.gpsimd.tensor_tensor(shared[:, 0, :], stage[:, BANK:T], windows[0][:, BANK:T], ALU.add)
 
         for n, c in enumerate((3, 1, 2)):
             for h in range(2):
-                bank = back_banks[(2 * n + h) % 4]
-                for kk in range(4):
+                cols = slice(h * BANK, (h + 1) * BANK)
+                bank = late_banks[(2 * n + h) % len(late_banks)]
+                for kk in range(BANK // P):
                     nc.tensor.transpose(bank[:, kk * P:(kk + 1) * P], faded[4 * h + kk][:, (c - 1) * P:c * P], ident[:])
-                result = sb.tile([P, BANK], F32, name="result%d_%d" % (c, h))
-                nc.vector.tensor_tensor(result[:], bank[:], windows[c][:, h * BANK:(h + 1) * BANK], ALU.add)
-                nc.sync.dma_start(out[c * P:(c + 1) * P, h * BANK:(h + 1) * BANK], result[:])
-
-        nc.gpsimd.tensor_tensor(stage, old_first[:], fade_wide[:], ALU.mult)
-        for h in range(2):
-            cols = slice(h * BANK, (h + 1) * BANK)
-            result = sb.tile([P, BANK], F32, name="result0_%d" % h)
-            nc.gpsimd.tensor_tensor(result[:], stage[:, cols], windows[0][:, cols], ALU.add)
-            nc.sync.dma_start(out[0:P, cols], result[:])
+                if (c, h) == (1, 1):
+                    nc.vector.tensor_tensor(shared[:, 1, :], bank[:], windows[c][:, cols], ALU.add)
+                    nc.sync.dma_start(out.rearrange("(c p) t -> p c t", p=P)[:, 0:2, cols], shared[:])
+                else:
+                    result = sb.tile([P, BANK], F32, name="result%d_%d" % (c, h))
+                    nc.vector.tensor_tensor(result[:], bank[:], windows[c][:, cols], ALU.add)
+                    nc.sync.dma_start(out[c * P:(c + 1) * P, cols], result[:])

from contextlib import ExitStack

import concourse.mybir as mybir
from concourse.masks import make_identity

D, E, T, I, Q = 512, 512, 1024, 256, 512
FLOPS = 2 * (2 * D * Q * I + Q * E * I)

F32 = mybir.dt.float32
BF16 = mybir.dt.bfloat16
I32 = mybir.dt.int32
U32 = mybir.dt.uint32
U16 = mybir.dt.uint16
U8 = mybir.dt.uint8
FP8X4 = mybir.dt.float8_e4m3fn_x4
ACT = mybir.ActivationFunctionType
ALU = mybir.AluOpType

P = 128
PACK = 4
BANK = 512
HALF = 256
TILES = E // P
TURNED = TILES - 1
BLOCKS = T // P
LINE = 4


def tile_attend_bgatedexp_b_v_kernel(tc, query, query2, keys_words, keys_scales, size, qs, grows, old, fade, offs, out):
    nc = tc.nc
    with ExitStack() as ctx:
        sb = ctx.enter_context(tc.tile_pool(name="sb", bufs=1))
        ps = ctx.enter_context(tc.psum_pool(name="ps", bufs=1))

        def load_half(src, h, name):
            raw = sb.tile([P, PACK, HALF], F32, name=name)
            nc.sync.dma_start(raw[:], src.rearrange("(p j) w -> p j w", j=PACK)[:, :, h * HALF:(h + 1) * HALF])
            return raw

        b_banks = [ps.tile([P, BANK], F32, name="b_bank%d" % n) for n in range(2)]
        a_banks = [ps.tile([P, BANK], F32, name="a_bank%d" % n) for n in range(PACK)]
        gv_banks = [ps.tile([P, BANK], F32, name="gv_bank%d" % n) for n in range(2)]

        pool_scales = sb.tile([P, T], U8, name="pool_scales", align_bytes=64)
        offsets = sb.tile([P, I // 16], U16, name="offsets")
        nc.sync.dma_start(offsets[:], offs)
        fade_runs = sb.tile([P, BLOCKS], F32, name="fade_runs")
        nc.sync.dma_start(fade_runs[:], fade.rearrange("o (p u) -> p (o u)", u=BLOCKS))
        pool_words = sb.tile([P, T], U32, name="pool_words", align_bytes=64)
        nc.sync.dma_start(pool_words[:].bitcast(I32), keys_words[0].rearrange("p n t -> p (n t)").bitcast(I32))
        for quad in range(4):
            nc.sync.dma_start(pool_scales[32 * quad:32 * quad + 32, :].bitcast(I32),
                              keys_scales[0, 4 * quad:4 * quad + 4, :].bitcast(I32).partition_broadcast(8))
        q2_raw = [load_half(query2, h, "q2_raw%d" % h) for h in range(2)]
        q_raw = [load_half(query, h, "q_raw%d" % h) for h in range(2)]
        size_pairs = sb.tile([P, 2], F32, name="size_pairs")
        nc.sync.dma_start(size_pairs[:], size.rearrange("o (p u) -> p (o u)", u=2))
        fade_rows = sb.tile([P, P], F32, name="fade_rows")
        nc.gpsimd.memset(fade_rows[:], 0.0)
        nc.sync.dma_start(fade_rows[0:BLOCKS, :], fade.rearrange("o (k p) -> (o k) p", p=P))
        qs_cols = sb.tile([P, PACK], F32, name="qs_cols")
        nc.sync.dma_start(qs_cols[:], qs.rearrange("(p r) o -> p (r o)", r=PACK))
        ident = sb.tile([P, P], F32, name="ident")
        make_identity(nc, ident[:])
        g_raw = [load_half(grows, h, "g_raw%d" % h) for h in range(2)]
        old_raw = []
        for j in range(T // HALF):
            chunk = sb.tile([P, TILES, HALF], F32, name="old_raw%d" % j, align_bytes=64)
            nc.sync.dma_start(chunk[:, 0:TURNED],
                              old.rearrange("(c p) t -> p c t", p=P)[:, 1:TILES, j * HALF:(j + 1) * HALF])
            old_raw.append(chunk)
        old_first = sb.tile([P, T], F32, name="old_first")
        nc.sync.dma_start(old_first[:], old[0:P, :])

        windows = []
        for c in range(TILES):
            window = sb.tile([P, T], F32, name="window%d" % c)
            (nc.vector if c < TILES // 2 else nc.gpsimd).memset(window[:], 0.0)
            windows.append(window)

        fade_wide = sb.tile([P, T], F32, name="fade_wide")
        for h in range(2):
            for u in range(4):
                nc.tensor.transpose(a_banks[h][:, u * P:(u + 1) * P],
                                    fade_runs[:, 4 * h + u:4 * h + u + 1].to_broadcast([P, P]), ident[:])
            nc.scalar.copy(fade_wide[:].rearrange("p (n h u) -> p h n u", h=2, u=4)[:, h],
                           a_banks[h][:].rearrange("p (u n) -> p n u", u=4))

        key_words = sb.tile([P, I], U32, name="key_words", align_bytes=64)
        key_scales = sb.tile([P, I], U8, name="key_scales", align_bytes=64)
        nc.vector.tensor_copy(key_words[:], pool_words[:].indirect(offsets[:]))
        nc.vector.tensor_copy(key_scales[:], pool_scales[:].indirect(offsets[:]))

        dealt = sb.tile([P, PACK, P, PACK], BF16, name="dealt", align_bytes=64)

        def scores(raw, name, outs):
            rows = HALF // PACK
            for h in range(2):
                nc.vector.tensor_copy(
                    dealt[:, :, h * rows:(h + 1) * rows, :].rearrange("p r s j -> p s j r"),
                    raw[h][:].rearrange("p j (s r) -> p s j r", r=PACK))
            for pair in range(2):
                codes = sb.tile([P, 2 * P], U32, name="%s_codes%d" % (name, pair), align_bytes=64)
                scales = sb.tile([P, 2 * P], U8, name="%s_scales%d" % (name, pair), align_bytes=64)
                nc.vector.quantize_mx(codes[:].bitcast(FP8X4), scales[:],
                                      dealt[:, 2 * pair:2 * pair + 2, :, :].rearrange("p r s j -> p (r s j)"))
                for u in range(2):
                    cols = slice(u * P, (u + 1) * P)
                    nc.tensor.matmul_mx(outs[2 * pair + u], lhsT=codes[:, cols].bitcast(FP8X4), lhsT_scale=scales[:, cols],
                                        rhs=key_words[:].bitcast(FP8X4), rhs_scale=key_scales[:], start=True, stop=True)

        gates = []
        scores(q2_raw, "b", [b_banks[r // 2][:, (r % 2) * I:(r % 2 + 1) * I] for r in range(PACK)])
        for pair in range(2):
            gate = sb.tile([P, 2 * I], F32, name="gate%d" % pair, align_bytes=64)
            nc.scalar.activation(gate[:], b_banks[pair][:], ACT.Sigmoid)
            gates.append(gate)

        for u in range(2):
            nc.tensor.transpose(b_banks[0][:, u * P:(u + 1) * P], size_pairs[:, u:u + 1].to_broadcast([P, P]), ident[:])
        nc.tensor.transpose(b_banks[1][:, 0:P], fade_rows[:], ident[:])

        scores(q_raw, "a", [a_banks[r][:, 0:I] for r in range(PACK)])
        wq = sb.tile([P, PACK, I], F32, name="wq")
        gv_all = sb.tile([P, TILES * I], F32, name="gv_all")
        gv = [gv_all[:, c * I:(c + 1) * I] for c in range(TILES)]
        neg_max = [sb.tile([P, 1], F32, name="neg_max%d" % r) for r in range(PACK - 1)] + [gv_all[:, 0:1]]
        expo = [sb.tile([P, I], F32, name="expo%d" % r) for r in range(PACK)]
        for r in range(PACK):
            nc.vector.tensor_reduce(neg_max[r][:], a_banks[r][:, 0:I], mybir.AxisListType.X, ALU.max, negate=True)
            nc.scalar.activation(expo[r][:], a_banks[r][:, 0:I], ACT.Exp, bias=neg_max[r][:])
        nc.scalar.copy(gv_all[:].rearrange("p (c i) -> p c i", c=TILES)[:, :, 0:BLOCKS // TILES],
                       b_banks[1][:, 0:BLOCKS].rearrange("p (j c) -> p c j", c=TILES))
        probs, row_sums = [], []
        for pair in range(2):
            row_sum = sb.tile([P, 2], F32, name="row_sum%d" % pair)
            prob = sb.tile([P, 2, I], F32, name="prob%d" % pair)
            for u in range(2):
                nc.vector.scalar_tensor_tensor(prob[:, u, :], expo[2 * pair + u][:], 1.0, gates[pair][:, u * I:(u + 1) * I],
                                               ALU.mult, ALU.mult, accum_out=row_sum[:, u:u + 1])
            probs.append(prob)
            row_sums.append(row_sum)
        for pair in range(2):
            inv = sb.tile([P, 2], F32, name="inv%d" % pair)
            nc.vector.reciprocal(inv[:], row_sums[pair][:])
            row_factor = sb.tile([P, 2], F32, name="row_factor%d" % pair)
            nc.vector.tensor_tensor(row_factor[:], inv[:], qs_cols[:, 2 * pair:2 * pair + 2], ALU.mult)
            for u in range(2):
                nc.vector.scalar_tensor_tensor(
                    wq[:, 2 * pair + u, :].rearrange("p (n u) -> p n u", u=2),
                    probs[pair][:, u, :].rearrange("p (n u) -> p n u", u=2),
                    row_factor[:, u:u + 1], b_banks[0][:, 0:I].rearrange("p (u n) -> p n u", u=2), ALU.mult, ALU.mult)

        def quantise_grows(h, grouped, copy):
            copy(grouped.rearrange("p (c i j) -> p c j i", i=LINE, j=PACK),
                 g_raw[h][:].rearrange("p j (c i) -> p c j i", i=LINE))
            codes = sb.tile([P, HALF], U32, name="g_codes%d" % h, align_bytes=64)
            scales = sb.tile([P, HALF], U8, name="g_scales%d" % h, align_bytes=64)
            nc.vector.quantize_mx(codes[:].bitcast(FP8X4), scales[:], grouped)
            return codes, scales

        g_quant = [quantise_grows(0, dealt[:, 2:4].rearrange("p r s j -> p (r s j)"), nc.vector.tensor_copy)]

        faded = []
        for k in range(BLOCKS):
            bank = a_banks[k % len(a_banks)]
            for c in range(TURNED):
                nc.tensor.transpose(bank[:, c * P:(c + 1) * P], old_raw[k // 2][:, c, (k % 2) * P:(k % 2 + 1) * P], ident[:])
            block = sb.tile([P, TURNED * P], F32, name="faded%d" % k)
            fade_col = gv[k % TILES][:, k // TILES:k // TILES + 1]
            nc.scalar.activation(block[:], bank[:, 0:TURNED * P], ACT.Copy, scale=fade_col)
            faded.append(block)

        stage = old_raw[-1][:].rearrange("p c t -> p (c t)")
        wq_grouped = stage[:, BANK:T].bitcast(BF16).rearrange("p (i r) -> p i r", r=PACK)
        nc.vector.tensor_copy(wq_grouped[:].rearrange("p (c i) r -> p c r i", i=LINE),
                              wq[:].rearrange("p r (c i) -> p c r i", i=LINE))
        wq_codes = sb.tile([P, I], U32, name="wq_codes", align_bytes=64)
        wq_scales = sb.tile([P, I], U8, name="wq_scales", align_bytes=64)
        nc.vector.quantize_mx(wq_codes[:].bitcast(FP8X4), wq_scales[:], wq_grouped[:].rearrange("p i r -> p (i r)"))
        g_quant.append(quantise_grows(1, stage[:, 0:BANK].bitcast(BF16), nc.scalar.copy))

        late_banks = [gv_banks[0], b_banks[1], gv_banks[1], b_banks[0]]
        gv_psum = [bank[:, 0:I] for bank in late_banks]
        for c in range(TILES):
            codes, scales = g_quant[c // 2]
            cols = slice((c % 2) * P, (c % 2 + 1) * P)
            nc.tensor.matmul_mx(gv_psum[c], lhsT=codes[:, cols].bitcast(FP8X4), lhsT_scale=scales[:, cols],
                                rhs=wq_codes[:].bitcast(FP8X4), rhs_scale=wq_scales[:], start=True, stop=True)
        for c in range(TILES):
            nc.vector.tensor_copy(gv[c], gv_psum[c])
            if c == TILES - 1:
                nc.vector.tensor_copy(windows[c][:].indirect(offsets[:]), gv[c])
            else:
                nc.scalar.activation(windows[c][:].indirect(offsets[:]), gv[c], ACT.Copy)

        shared = sb.tile([P, 2, BANK], F32, name="shared")
        first_half = sb.tile([P, BANK], F32, name="first_half")
        nc.gpsimd.tensor_tensor(stage, old_first[:], fade_wide[:], ALU.mult)
        nc.gpsimd.tensor_tensor(first_half[:], stage[:, 0:BANK], windows[0][:, 0:BANK], ALU.add)
        nc.sync.dma_start(out[0:P, 0:BANK], first_half[:])
        nc.gpsimd.tensor_tensor(shared[:, 0, :], stage[:, BANK:T], windows[0][:, BANK:T], ALU.add)

        for n, c in enumerate((3, 1, 2)):
            for h in range(2):
                cols = slice(h * BANK, (h + 1) * BANK)
                bank = late_banks[(2 * n + h) % len(late_banks)]
                for kk in range(BANK // P):
                    nc.tensor.transpose(bank[:, kk * P:(kk + 1) * P], faded[4 * h + kk][:, (c - 1) * P:c * P], ident[:])
                if (c, h) == (1, 1):
                    nc.vector.tensor_tensor(shared[:, 1, :], bank[:], windows[c][:, cols], ALU.add)
                    nc.sync.dma_start(out.rearrange("(c p) t -> p c t", p=P)[:, 0:2, cols], shared[:])
                else:
                    result = sb.tile([P, BANK], F32, name="result%d_%d" % (c, h))
                    nc.vector.tensor_tensor(result[:], bank[:], windows[c][:, cols], ALU.add)
                    nc.sync.dma_start(out[c * P:(c + 1) * P, cols], result[:])
